import numpy as np
import ml_dtypes


def mxq(x, axis, fmt="e4m3"):
    dtype, down = {"e4m3": (ml_dtypes.float8_e4m3fn, 7), "e5m2": (ml_dtypes.float8_e5m2, 14)}[fmt]
    v = np.moveaxis(np.asarray(x, np.float32).astype(ml_dtypes.bfloat16).astype(np.float64), axis, -1)
    blocks = v.reshape(v.shape[:-1] + (-1, 32))
    amax = np.abs(blocks).max(-1, keepdims=True)
    byte = np.maximum(np.where(amax > 0, np.frexp(amax)[1] - 1 + 127, 0) - down, 1)
    scale = np.exp2(byte - 127.0)
    codes = (blocks / scale).astype(np.float32).astype(dtype).astype(np.float64)
    return np.moveaxis((codes * scale).reshape(v.shape), -1, axis)


WIDE = False


def mx_kscale(k):
    if not WIDE:
        return np.ones(k)
    levels = np.array([10, -10, 5, -5, 0])
    if k % 512:
        return np.exp2(np.random.permutation(np.resize(levels, k // 32))).repeat(32)
    a = np.empty((k // 512, 16))
    for p in range(k // 512):
        a[p, :8] = np.random.permutation(np.resize(levels, 8))
        for g in range(8):
            far = levels[np.abs(levels - a[p, g]) >= 10]
            a[p, g + 8] = far[np.random.randint(len(far))]
    return np.exp2(a.ravel()).repeat(32)


def f64(x):
    return np.asarray(x).astype(np.float64)


def striped(idx):
    return np.tile(idx.reshape(-1, 16).T, (8, 1)).astype(np.uint16)


def unstriped(offs):
    return offs[:16].T.reshape(-1).astype(np.int64)


def striped8(idx):
    return np.concatenate([x.reshape(-1, 16).T for x in idx]).astype(np.uint16)


def runs(offs, k):
    lists = np.stack([offs[16 * r : 16 * r + 16].T.reshape(-1) for r in range(8)]).astype(np.int64)
    return lists[np.arange(k) % 512 // 64]


def pack_weight(w):
    k, n = w.shape
    w = f64(np.asarray(w, np.float32).astype(ml_dtypes.bfloat16)).reshape(k // 32, 32, n)
    amax = np.abs(w).max(1)
    byte = np.clip(np.where(amax > 0, np.frexp(amax)[1] - 1 + 127 - 7, 1), 1, 254)
    scaled = (w * np.exp2(127.0 - byte)[:, None, :]).reshape(k, n).astype(np.float32)
    words = np.ascontiguousarray(scaled.reshape(k // 512, 128, 4, n).transpose(0, 1, 3, 2)).astype(ml_dtypes.float8_e4m3fn).view(np.uint8)
    return words, np.ascontiguousarray(byte.astype(np.uint8).reshape(k // 512, 16, n))


def unpack_weight(words, scales):
    g, p, n, _ = words.shape
    vals = np.ascontiguousarray(words).view(ml_dtypes.float8_e4m3fn).astype(np.float64) * np.repeat(np.exp2(scales.astype(np.float64) - 127.0), 8, axis=1)[..., None]
    return vals.transpose(0, 1, 3, 2).reshape(g * 512, n)

def planes(y):
    n, m = y.shape
    v = y.astype(np.float32).astype(ml_dtypes.bfloat16).astype(np.float64).reshape(n // 32, 32, m)
    top = np.abs(v).max(1)
    byte = np.clip(np.where(top > 0, np.frexp(top)[1] - 1 + 127 - 7, 1), 1, 254)
    codes = (v * np.exp2(127.0 - byte)[:, None, :]).reshape(n, m).astype(np.float32).astype(ml_dtypes.float8_e4m3fn).view(np.uint8)
    words = codes.reshape(n // 512, 128, 4, m).transpose(0, 1, 3, 2)
    return np.ascontiguousarray(words), np.ascontiguousarray(byte.astype(np.uint8).reshape(n // 512, 16, m))


K, T, S, N, H = 512, 2048, 512, 512, 512


def setup_inputs():
    n = np.random.standard_normal
    s = mx_kscale(K)[:, None]
    u = mx_kscale(H)
    packed_xT = pack_weight(n((K, T)) * s)
    packed_w1 = pack_weight(n((K, H)) / np.sqrt(K) / s)
    packed_w2 = pack_weight(n((K, H)) / np.sqrt(K) / s)
    packed_w3 = pack_weight(n((H, N)) / np.sqrt(H) / u[:, None])
    return {
        "x_words": packed_xT[0],
        "x_scales": packed_xT[1],
        "w1_words": packed_w1[0],
        "w1_scales": packed_w1[1],
        "w2_words": packed_w2[0],
        "w2_scales": packed_w2[1],
        "gn": (np.random.uniform(0.5, 1.5, (H, 1)) * u[:, None]).astype(np.float32),
        "w3_words": packed_w3[0],
        "w3_scales": packed_w3[1],
        "offs": striped(np.random.permutation(T)[:S]),
        "two": striped(np.random.permutation(T)[:S]),
        "n1": striped8(np.stack([np.random.permutation(S) for _ in range(8)])),
        "n2": striped8(np.stack([np.random.permutation(S) for _ in range(8)])),
        "n3": striped8(np.stack([np.random.permutation(S) for _ in range(8)])),
        "n4": striped8(np.stack([np.random.permutation(S) for _ in range(8)])),
        "n5": striped8(np.stack([np.random.permutation(S) for _ in range(8)])),
        "n6": striped8(np.stack([np.random.permutation(S) for _ in range(8)])),
    }


def reference(x_words, x_scales, w1_words, w1_scales, w2_words, w2_scales, gn, w3_words, w3_scales, offs, two, n1, n2, n3, n4, n5, n6):
    xq = unpack_weight(x_words, x_scales)[:, unstriped(offs)]
    y = unpack_weight(w1_words, w1_scales).T @ xq
    x_two = unpack_weight(x_words, x_scales)[:, unstriped(two)]
    d = unpack_weight(w2_words, w2_scales).T @ x_two
    z = f64(gn) * (np.maximum(y[np.arange(H)[:, None], runs(n1, H)] + d[np.arange(H)[:, None], runs(n3, H)], y[np.arange(H)[:, None], runs(n2, H)] + d[np.arange(H)[:, None], runs(n4, H)]))
    h = unpack_weight(w3_words, w3_scales).T @ mxq(z, 0, "e4m3")
    st = np.maximum(h, h[np.arange(N)[:, None], runs(n5, N)])
    out_0 = np.minimum(st, st[np.arange(N)[:, None], runs(n6, N)])
    return (out_0,) + planes(out_0)

@@ -1,0 +1,186 @@
+from contextlib import ExitStack
+
+import concourse.mybir as mybir
+
+K, T, S, N, H = 512, 2048, 512, 512, 512
+FLOPS = 2 * K * H * S * 2 + 2 * H * N * S
+
+F32 = mybir.dt.float32
+BF16 = mybir.dt.bfloat16
+I32 = mybir.dt.int32
+U32 = mybir.dt.uint32
+U16 = mybir.dt.uint16
+U8 = mybir.dt.uint8
+FP8X4 = mybir.dt.float8_e4m3fn_x4
+ADD = mybir.AluOpType.add
+MAX = mybir.AluOpType.max
+MIN = mybir.AluOpType.min
+COPY = mybir.ActivationFunctionType.Copy
+
+P = 128
+PACK = 4
+PER_COL = 16
+Z_CHUNKS = ((0, 256), (256, 384), (384, 512))
+OUT_CHUNKS = ((0, 384), (384, 512))
+
+
+def entries(lst, lo, hi):
+    return lst[:, lo // PER_COL : hi // PER_COL]
+
+
+def tile_picked_twlpathbhopmn_none_po_kernel(
+    tc, x_words, x_scales, w1_words, w1_scales, w2_words, w2_scales, gn, w3_words, w3_scales,
+    offs, two, n1, n2, n3, n4, n5, n6, out_0, out_1, out_2,
+):
+    nc = tc.nc
+    with ExitStack() as ctx:
+        sb = ctx.enter_context(tc.tile_pool(name="sb", bufs=1))
+        ps = ctx.enter_context(tc.psum_pool(name="ps", bufs=1))
+
+        def load_words(src, width, name):
+            dst = sb.tile([P, width], U32, name=name, align_bytes=64)
+            nc.sync.dma_start(dst[:].bitcast(I32), src[0].rearrange("p n t -> p (n t)").bitcast(I32))
+            return dst
+
+        def load_scale_rows(queue, dst, src, first):
+            for q in range(4):
+                queue.dma_start(dst[32 * q + first : 32 * q + first + 4, :].bitcast(I32), src[0, 4 * q : 4 * q + 4, :].bitcast(I32))
+
+        def load_list(src, name):
+            dst = sb.tile([P, S // PER_COL], U16, name=name)
+            nc.sync.dma_start(dst[:], src)
+            return dst
+
+        def deal(src, dtype, name):
+            dst = sb.tile([P, H], dtype, name=name, align_bytes=64)
+            nc.vector.tensor_copy(dst[:].rearrange("p (t m) -> p m t", t=PACK), src[:].rearrange("p (m t) -> p m t", t=PACK))
+            return dst
+
+        xs = sb.tile([P, T], U8, name="xs", align_bytes=64)
+        ws = sb.tile([P, H], U8, name="ws", align_bytes=64)
+        nc.vector.memset(xs[:].bitcast(I32), 0)
+        nc.gpsimd.memset(ws[:].bitcast(I32), 0)
+
+        l_offs = load_list(offs, "l_offs")
+        w1 = load_words(w1_words, H, "w1")
+        load_scale_rows(nc.scalar, xs, x_scales, 0)
+        l_two = load_list(two, "l_two")
+        xw = load_words(x_words, T, "xw")
+        load_scale_rows(nc.gpsimd, ws, w3_scales, 8)
+        load_scale_rows(nc.scalar, ws, w1_scales, 0)
+        load_scale_rows(nc.scalar, ws, w2_scales, 4)
+        w2 = load_words(w2_words, H, "w2")
+        l1 = load_list(n1, "l1")
+        l2 = load_list(n2, "l2")
+        l3 = load_list(n3, "l3")
+        l4 = load_list(n4, "l4")
+        gain = sb.tile([P, PACK], F32, name="gain")
+        nc.sync.dma_start(gain[:], gn.rearrange("(p t) o -> p (t o)", t=PACK))
+        w3 = load_words(w3_words, N, "w3")
+        l5 = load_list(n5, "l5")
+        l6 = load_list(n6, "l6")
+
+        def pick(window, lst, dtype, name):
+            dst = sb.tile([P, S], dtype, name=name, align_bytes=64)
+            nc.vector.tensor_copy(dst[:], window[:].indirect(lst[:]))
+            return dst
+
+        def product(bank, w_codes, w_plane, first, t, codes, plane, lo, hi):
+            cols = slice(P * t, P * (t + 1))
+            nc.tensor.matmul_mx(
+                out=bank[:, lo:hi], lhsT=w_codes[:, cols].bitcast(FP8X4), lhsT_scale=w_plane[first:P, cols],
+                rhs=codes[:, lo:hi].bitcast(FP8X4), rhs_scale=plane[:, lo:hi], start=True, stop=True,
+            )
+
+        def layer(w_codes, first, codes, plane, name, window):
+            rows = []
+            for t in range(PACK):
+                bank = ps.tile([P, S], F32, name=name + "_bank%d" % t)
+                product(bank, w_codes, wsd, first, t, codes, plane, 0, S)
+                row = sb.tile([P, window], F32, name=name + "%d" % t)
+                nc.scalar.copy(row[:, 0:S], bank[:])
+                rows.append(row)
+            return rows
+
+        w1d = deal(w1, U32, "w1d")
+        xs_a = pick(xs, l_offs, U8, "xs_a")
+        xs_b = pick(xs, l_two, U8, "xs_b")
+        xw_a = pick(xw, l_offs, U32, "xw_a")
+        wsd = deal(ws, U8, "wsd")
+        y = layer(w1d, 0, xw_a, xs_a, "y", 2 * S)
+        xw_b = pick(xw, l_two, U32, "xw_b")
+        w2d = deal(w2, U32, "w2d")
+        d = layer(w2d, 4, xw_b, xs_b, "d", S)
+
+        y1 = [sb.tile([P, S], F32, name="y1_%d" % t) for t in range(PACK)]
+        y2 = [sb.tile([P, S], F32, name="y2_%d" % t) for t in range(PACK)]
+        for t in range(PACK):
+            nc.vector.tensor_copy(y1[t][:], y[t][:].indirect(l1[:]))
+            nc.vector.tensor_copy(y2[t][:], y[t][:].indirect(l2[:]))
+        w3d = deal(w3, U32, "w3d")
+
+        zq = sb.tile([P, S], U32, name="zq", align_bytes=64)
+        zs = sb.tile([P, S], U8, name="zs", align_bytes=64)
+        h_banks = [ps.tile([P, S], F32, name="y_bank%d" % t) for t in range(PACK)]
+        h = [sb.tile([P, 2 * S], F32, name="h%d" % t) for t in range(PACK)]
+        for c, (lo, hi) in enumerate(Z_CHUNKS):
+            width = hi - lo
+            zb = sb.tile([P, width, PACK], BF16, name="zb%d" % c, align_bytes=64)
+            s1 = sb.tile([P, PACK, width], F32, name="s1_%d" % c)
+            s2 = sb.tile([P, PACK, width], F32, name="s2_%d" % c)
+            big = sb.tile([P, PACK, width], F32, name="big_%d" % c)
+            together = 1 if hi == S else PACK
+            for t in range(PACK + 1):
+                if t < PACK:
+                    nc.vector.tensor_tensor(s1[:, t, :], d[t][:].indirect(entries(l3, lo, hi)), y1[t][:, lo:hi], ADD)
+                    nc.vector.tensor_tensor(s2[:, t, :], d[t][:].indirect(entries(l4, lo, hi)), y2[t][:, lo:hi], ADD)
+                if t > 0 and t % together == 0:
+                    group = slice(t - together, t)
+                    nc.vector.tensor_tensor(big[:, group, :], s1[:, group, :], s2[:, group, :], MAX)
+                    for u in range(t - together, t):
+                        nc.scalar.activation(zb[:, :, u], big[:, u, :], COPY, scale=gain[:, u : u + 1])
+            nc.vector.quantize_mx(out=zq[:, lo:hi].bitcast(FP8X4), scales=zs[:, lo:hi], in_=zb[:].rearrange("p c t -> p (c t)"))
+            for t in range(PACK):
+                product(h_banks[t], w3d, wsd, 8, t, zq, zs, lo, hi)
+                nc.scalar.copy(h[t][:, lo:hi], h_banks[t][:, lo:hi])
+
+        st = [sb.tile([P, S], F32, name="st%d" % t) for t in range(PACK)]
+        h5 = [sb.tile([P, S], F32, name="h5_%d" % t) for t in range(PACK)]
+        for t in range(PACK + 1):
+            if t < PACK:
+                nc.vector.tensor_copy(h5[t][:], h[t][:].indirect(l5[:]))
+            if t > 0:
+                nc.vector.tensor_tensor(st[t - 1][:], h5[t - 1][:], h[t - 1][:, 0:S], MAX)
+
+        oq = sb.tile([P, S], U32, name="oq", align_bytes=64)
+        osc = sb.tile([P, S], U8, name="osc", align_bytes=64)
+        out_rows = out_0.rearrange("(p t) j -> p t j", t=PACK)
+        out_words = out_1[0].rearrange("p n t -> p (n t)").bitcast(I32)
+        for c, (lo, hi) in enumerate(OUT_CHUNKS):
+            width = hi - lo
+            last = c == len(OUT_CHUNKS) - 1
+            st6 = sb.tile([P, PACK, width], F32, name="st6_%d" % c)
+            res = sb.tile([P, PACK, width], F32, name="res%d" % c)
+            for t in range(PACK + 1):
+                if t < PACK:
+                    nc.vector.tensor_copy(st6[:, t, :], st[t][:].indirect(entries(l6, lo, hi)))
+                if t > 0:
+                    nc.vector.tensor_tensor(res[:, t - 1, :], st6[:, t - 1, :], st[t - 1][:, lo:hi], MIN)
+            nc.sync.dma_start(out_rows[:, :, lo:hi], res[:])
+            ob = sb.tile([P, width, PACK], BF16, name="ob%d" % c, align_bytes=64)
+            woven = ob[:].rearrange("p (c i) t -> p c t i", i=4)
+            planes = res[:].rearrange("p t (c i) -> p c t i", i=4)
+            if last:
+                nc.vector.tensor_copy(woven, planes)
+            else:
+                nc.scalar.copy(woven, planes)
+            for a in range(0, width, 256):
+                b = min(a + 256, width)
+                nc.vector.quantize_mx(
+                    out=oq[:, lo + a : lo + b].bitcast(FP8X4), scales=osc[:, lo + a : lo + b],
+                    in_=ob[:, a:b, :].rearrange("p c t -> p (c t)"),
+                )
+            nc.sync.dma_start(out_words[:, lo:hi], oq[:, lo:hi].bitcast(I32))
+        for q in range(4):
+            queue = nc.scalar if q % 2 == 0 else nc.sync
+            queue.dma_start(out_2[0, 4 * q : 4 * q + 4, :].bitcast(I32), osc[32 * q : 32 * q + 4, :].bitcast(I32))

@@ -20,12 +20,16 @@ COPY = mybir.ActivationFunctionType.Copy
 P = 128
 PACK = 4
 PER_COL = 16
-Z_CHUNKS = ((0, 256), (256, 384), (384, 512))
+Z_CHUNKS = ((0, 384), (384, 512))
 OUT_CHUNKS = ((0, 384), (384, 512))
 
 
 def entries(lst, lo, hi):
     return lst[:, lo // PER_COL : hi // PER_COL]
+
+
+def pieces(lo, hi):
+    return [(a, min(a + 256, hi)) for a in range(lo, hi, 256)]
 
 
 def tile_picked_twlpathbhopmn_none_po_kernel(
@@ -51,27 +55,34 @@ def tile_picked_twlpathbhopmn_none_po_kernel(
             nc.sync.dma_start(dst[:], src)
             return dst
 
+        def deal_aside(src, dtype, name):
+            dst = sb.tile([P, H], dtype, name=name, align_bytes=64)
+            nc.gpsimd.tensor_copy(dst[:].rearrange("p (t m) -> p t m", t=PACK), src[:].rearrange("p (m t) -> p t m", t=PACK))
+            return dst
+
         def deal(src, dtype, name):
             dst = sb.tile([P, H], dtype, name=name, align_bytes=64)
             nc.vector.tensor_copy(dst[:].rearrange("p (t m) -> p m t", t=PACK), src[:].rearrange("p (m t) -> p m t", t=PACK))
             return dst
 
         xs = sb.tile([P, T], U8, name="xs", align_bytes=64)
-        ws = sb.tile([P, H], U8, name="ws", align_bytes=64)
+        ws1 = sb.tile([P, H], U8, name="ws1", align_bytes=64)
+        ws23 = sb.tile([P, H], U8, name="ws23", align_bytes=64)
         nc.vector.memset(xs[:].bitcast(I32), 0)
-        nc.gpsimd.memset(ws[:].bitcast(I32), 0)
+        nc.gpsimd.memset(ws1[:].bitcast(I32), 0)
+        nc.gpsimd.memset(ws23[:].bitcast(I32), 0)
 
         l_offs = load_list(offs, "l_offs")
         w1 = load_words(w1_words, H, "w1")
-        load_scale_rows(nc.scalar, xs, x_scales, 0)
         l_two = load_list(two, "l_two")
+        load_scale_rows(nc.sync, xs, x_scales, 0)
         xw = load_words(x_words, T, "xw")
-        load_scale_rows(nc.gpsimd, ws, w3_scales, 8)
-        load_scale_rows(nc.scalar, ws, w1_scales, 0)
-        load_scale_rows(nc.scalar, ws, w2_scales, 4)
-        w2 = load_words(w2_words, H, "w2")
+        load_scale_rows(nc.sync, ws1, w1_scales, 0)
         l1 = load_list(n1, "l1")
         l2 = load_list(n2, "l2")
+        w2 = load_words(w2_words, H, "w2")
+        load_scale_rows(nc.sync, ws23, w2_scales, 0)
+        load_scale_rows(nc.sync, ws23, w3_scales, 4)
         l3 = load_list(n3, "l3")
         l4 = load_list(n4, "l4")
         gain = sb.tile([P, PACK], F32, name="gain")
@@ -92,32 +103,41 @@ def tile_picked_twlpathbhopmn_none_po_kernel(
                 rhs=codes[:, lo:hi].bitcast(FP8X4), rhs_scale=plane[:, lo:hi], start=True, stop=True,
             )
 
-        def layer(w_codes, first, codes, plane, name, window):
+        def quantise(codes, plane, woven, lo, hi):
+            for a, b in pieces(lo, hi):
+                nc.vector.quantize_mx(
+                    out=codes[:, a:b].bitcast(FP8X4), scales=plane[:, a:b],
+                    in_=woven[:, a - lo : b - lo, :].rearrange("p c t -> p (c t)"),
+                )
+
+        def layer(w_codes, w_plane, codes, plane, name, windows):
             rows = []
             for t in range(PACK):
                 bank = ps.tile([P, S], F32, name=name + "_bank%d" % t)
-                product(bank, w_codes, wsd, first, t, codes, plane, 0, S)
-                row = sb.tile([P, window], F32, name=name + "%d" % t)
-                nc.scalar.copy(row[:, 0:S], bank[:])
-                rows.append(row)
+                product(bank, w_codes, w_plane, 0, t, codes, plane, 0, S)
+                copies = [sb.tile([P, w], F32, name=name + "%d_%d" % (t, w)) for w in windows]
+                for row in copies:
+                    nc.scalar.copy(row[:, 0:S], bank[:])
+                rows.append(copies)
             return rows
 
         w1d = deal(w1, U32, "w1d")
         xs_a = pick(xs, l_offs, U8, "xs_a")
         xs_b = pick(xs, l_two, U8, "xs_b")
         xw_a = pick(xw, l_offs, U32, "xw_a")
-        wsd = deal(ws, U8, "wsd")
-        y = layer(w1d, 0, xw_a, xs_a, "y", 2 * S)
+        ws1d = deal_aside(ws1, U8, "ws1d")
+        y = layer(w1d, ws1d, xw_a, xs_a, "y", (2 * S,))
         xw_b = pick(xw, l_two, U32, "xw_b")
-        w2d = deal(w2, U32, "w2d")
-        d = layer(w2d, 4, xw_b, xs_b, "d", S)
+        w2d = deal_aside(w2, U32, "w2d")
+        ws23d = deal_aside(ws23, U8, "ws23d")
+        d = layer(w2d, ws23d, xw_b, xs_b, "d", (2 * S, S))
 
+        w3d = deal_aside(w3, U32, "w3d")
         y1 = [sb.tile([P, S], F32, name="y1_%d" % t) for t in range(PACK)]
         y2 = [sb.tile([P, S], F32, name="y2_%d" % t) for t in range(PACK)]
         for t in range(PACK):
-            nc.vector.tensor_copy(y1[t][:], y[t][:].indirect(l1[:]))
-            nc.vector.tensor_copy(y2[t][:], y[t][:].indirect(l2[:]))
-        w3d = deal(w3, U32, "w3d")
+            nc.vector.tensor_copy(y1[t][:], y[t][0][:].indirect(l1[:]))
+            nc.vector.tensor_copy(y2[t][:], y[t][0][:].indirect(l2[:]))
 
         zq = sb.tile([P, S], U32, name="zq", align_bytes=64)
         zs = sb.tile([P, S], U8, name="zs", align_bytes=64)
@@ -129,19 +149,18 @@ def tile_picked_twlpathbhopmn_none_po_kernel(
             s1 = sb.tile([P, PACK, width], F32, name="s1_%d" % c)
             s2 = sb.tile([P, PACK, width], F32, name="s2_%d" % c)
             big = sb.tile([P, PACK, width], F32, name="big_%d" % c)
-            together = 1 if hi == S else PACK
             for t in range(PACK + 1):
                 if t < PACK:
-                    nc.vector.tensor_tensor(s1[:, t, :], d[t][:].indirect(entries(l3, lo, hi)), y1[t][:, lo:hi], ADD)
-                    nc.vector.tensor_tensor(s2[:, t, :], d[t][:].indirect(entries(l4, lo, hi)), y2[t][:, lo:hi], ADD)
-                if t > 0 and t % together == 0:
-                    group = slice(t - together, t)
-                    nc.vector.tensor_tensor(big[:, group, :], s1[:, group, :], s2[:, group, :], MAX)
-                    for u in range(t - together, t):
-                        nc.scalar.activation(zb[:, :, u], big[:, u, :], COPY, scale=gain[:, u : u + 1])
-            nc.vector.quantize_mx(out=zq[:, lo:hi].bitcast(FP8X4), scales=zs[:, lo:hi], in_=zb[:].rearrange("p c t -> p (c t)"))
+                    nc.vector.tensor_tensor(s1[:, t, :], d[t][c][:].indirect(entries(l3, lo, hi)), y1[t][:, lo:hi], ADD)
+                    nc.vector.tensor_tensor(s2[:, t, :], d[t][c][:].indirect(entries(l4, lo, hi)), y2[t][:, lo:hi], ADD)
+                if t > 0:
+                    u = t - 1
+                    nc.vector.tensor_tensor(big[:, u, :], s1[:, u, :], s2[:, u, :], MAX)
+                    nc.scalar.activation(zb[:, :, u], big[:, u, :], COPY, scale=gain[:, u : u + 1])
+            quantise(zq, zs, zb, lo, hi)
             for t in range(PACK):
-                product(h_banks[t], w3d, wsd, 8, t, zq, zs, lo, hi)
+                for a, b in pieces(lo, hi):
+                    product(h_banks[t], w3d, ws23d, 4, t, zq, zs, a, b)
                 nc.scalar.copy(h[t][:, lo:hi], h_banks[t][:, lo:hi])
 
         st = [sb.tile([P, S], F32, name="st%d" % t) for t in range(PACK)]
@@ -158,28 +177,18 @@ def tile_picked_twlpathbhopmn_none_po_kernel(
         out_words = out_1[0].rearrange("p n t -> p (n t)").bitcast(I32)
         for c, (lo, hi) in enumerate(OUT_CHUNKS):
             width = hi - lo
-            last = c == len(OUT_CHUNKS) - 1
             st6 = sb.tile([P, PACK, width], F32, name="st6_%d" % c)
             res = sb.tile([P, PACK, width], F32, name="res%d" % c)
+            ob = sb.tile([P, width, PACK], BF16, name="ob%d" % c, align_bytes=64)
             for t in range(PACK + 1):
                 if t < PACK:
                     nc.vector.tensor_copy(st6[:, t, :], st[t][:].indirect(entries(l6, lo, hi)))
                 if t > 0:
                     nc.vector.tensor_tensor(res[:, t - 1, :], st6[:, t - 1, :], st[t - 1][:, lo:hi], MIN)
+                if t > 0 and t % 2 == 0:
+                    nc.scalar.copy(ob[:, :, t - 2 : t], res[:, t - 2 : t, :].rearrange("p t c -> p c t"))
             nc.sync.dma_start(out_rows[:, :, lo:hi], res[:])
-            ob = sb.tile([P, width, PACK], BF16, name="ob%d" % c, align_bytes=64)
-            woven = ob[:].rearrange("p (c i) t -> p c t i", i=4)
-            planes = res[:].rearrange("p t (c i) -> p c t i", i=4)
-            if last:
-                nc.vector.tensor_copy(woven, planes)
-            else:
-                nc.scalar.copy(woven, planes)
-            for a in range(0, width, 256):
-                b = min(a + 256, width)
-                nc.vector.quantize_mx(
-                    out=oq[:, lo + a : lo + b].bitcast(FP8X4), scales=osc[:, lo + a : lo + b],
-                    in_=ob[:, a:b, :].rearrange("p c t -> p (c t)"),
-                )
+            quantise(oq, osc, ob, lo, hi)
             nc.sync.dma_start(out_words[:, lo:hi], oq[:, lo:hi].bitcast(I32))
         for q in range(4):
             queue = nc.scalar if q % 2 == 0 else nc.sync

@@ -13,6 +13,8 @@ U16 = mybir.dt.uint16
 U8 = mybir.dt.uint8
 FP8X4 = mybir.dt.float8_e4m3fn_x4
 ADD = mybir.AluOpType.add
+SUB = mybir.AluOpType.subtract
+RELU = mybir.ActivationFunctionType.Relu
 MAX = mybir.AluOpType.max
 MIN = mybir.AluOpType.min
 COPY = mybir.ActivationFunctionType.Copy
@@ -20,8 +22,10 @@ COPY = mybir.ActivationFunctionType.Copy
 P = 128
 PACK = 4
 PER_COL = 16
-Z_CHUNKS = ((0, 384), (384, 512))
-OUT_CHUNKS = ((0, 384), (384, 512))
+CUT = 384
+PARTS = ((0, CUT), (CUT, S))
+OUT_STEPS = tuple((t, lo, hi) for lo, hi in PARTS for t in range(PACK))
+H_ORDER = (2, 3, 0, 1)
 
 
 def entries(lst, lo, hi):
@@ -67,10 +71,12 @@ def tile_picked_twlpathbhopmn_none_po_kernel(
 
         xs = sb.tile([P, T], U8, name="xs", align_bytes=64)
         ws1 = sb.tile([P, H], U8, name="ws1", align_bytes=64)
-        ws23 = sb.tile([P, H], U8, name="ws23", align_bytes=64)
+        ws2 = sb.tile([P, H], U8, name="ws2", align_bytes=64)
+        ws3 = sb.tile([P, N], U8, name="ws3", align_bytes=64)
         nc.vector.memset(xs[:].bitcast(I32), 0)
         nc.gpsimd.memset(ws1[:].bitcast(I32), 0)
-        nc.gpsimd.memset(ws23[:].bitcast(I32), 0)
+        nc.gpsimd.memset(ws2[:].bitcast(I32), 0)
+        nc.gpsimd.memset(ws3[:].bitcast(I32), 0)
 
         l_offs = load_list(offs, "l_offs")
         w1 = load_words(w1_words, H, "w1")
@@ -79,15 +85,15 @@ def tile_picked_twlpathbhopmn_none_po_kernel(
         xw = load_words(x_words, T, "xw")
         load_scale_rows(nc.sync, ws1, w1_scales, 0)
         l1 = load_list(n1, "l1")
-        l2 = load_list(n2, "l2")
         w2 = load_words(w2_words, H, "w2")
-        load_scale_rows(nc.sync, ws23, w2_scales, 0)
-        load_scale_rows(nc.sync, ws23, w3_scales, 4)
+        load_scale_rows(nc.sync, ws2, w2_scales, 0)
         l3 = load_list(n3, "l3")
+        l2 = load_list(n2, "l2")
         l4 = load_list(n4, "l4")
         gain = sb.tile([P, PACK], F32, name="gain")
         nc.sync.dma_start(gain[:], gn.rearrange("(p t) o -> p (t o)", t=PACK))
         w3 = load_words(w3_words, N, "w3")
+        load_scale_rows(nc.sync, ws3, w3_scales, 0)
         l5 = load_list(n5, "l5")
         l6 = load_list(n6, "l6")
 
@@ -115,7 +121,7 @@ def tile_picked_twlpathbhopmn_none_po_kernel(
             for t in range(PACK):
                 bank = ps.tile([P, S], F32, name=name + "_bank%d" % t)
                 product(bank, w_codes, w_plane, 0, t, codes, plane, 0, S)
-                copies = [sb.tile([P, w], F32, name=name + "%d_%d" % (t, w)) for w in windows]
+                copies = [sb.tile([P, w], F32, name=name + "%d_%d" % (t, w)) for w in windows[t]]
                 for row in copies:
                     nc.scalar.copy(row[:, 0:S], bank[:])
                 rows.append(copies)
@@ -126,70 +132,122 @@ def tile_picked_twlpathbhopmn_none_po_kernel(
         xs_b = pick(xs, l_two, U8, "xs_b")
         xw_a = pick(xw, l_offs, U32, "xw_a")
         ws1d = deal_aside(ws1, U8, "ws1d")
-        y = layer(w1d, ws1d, xw_a, xs_a, "y", (2 * S,))
+        y = layer(w1d, ws1d, xw_a, xs_a, "y", [(2 * S,)] * PACK)
         xw_b = pick(xw, l_two, U32, "xw_b")
         w2d = deal_aside(w2, U32, "w2d")
-        ws23d = deal_aside(ws23, U8, "ws23d")
-        d = layer(w2d, ws23d, xw_b, xs_b, "d", (2 * S, S))
+        ws2d = deal_aside(ws2, U8, "ws2d")
+        d = layer(w2d, ws2d, xw_b, xs_b, "d", [(2 * S,), (2 * S,), (2 * S, S), (2 * S, S)])
 
         w3d = deal_aside(w3, U32, "w3d")
-        y1 = [sb.tile([P, S], F32, name="y1_%d" % t) for t in range(PACK)]
-        y2 = [sb.tile([P, S], F32, name="y2_%d" % t) for t in range(PACK)]
-        for t in range(PACK):
-            nc.vector.tensor_copy(y1[t][:], y[t][0][:].indirect(l1[:]))
-            nc.vector.tensor_copy(y2[t][:], y[t][0][:].indirect(l2[:]))
-
+        ws3d = deal_aside(ws3, U8, "ws3d")
         zq = sb.tile([P, S], U32, name="zq", align_bytes=64)
         zs = sb.tile([P, S], U8, name="zs", align_bytes=64)
+        zb = [sb.tile([P, hi - lo, PACK], BF16, name="zb%d" % lo, align_bytes=64) for lo, hi in PARTS]
         h_banks = [ps.tile([P, S], F32, name="y_bank%d" % t) for t in range(PACK)]
         h = [sb.tile([P, 2 * S], F32, name="h%d" % t) for t in range(PACK)]
-        for c, (lo, hi) in enumerate(Z_CHUNKS):
-            width = hi - lo
-            zb = sb.tile([P, width, PACK], BF16, name="zb%d" % c, align_bytes=64)
-            s1 = sb.tile([P, PACK, width], F32, name="s1_%d" % c)
-            s2 = sb.tile([P, PACK, width], F32, name="s2_%d" % c)
-            big = sb.tile([P, PACK, width], F32, name="big_%d" % c)
-            for t in range(PACK + 1):
-                if t < PACK:
-                    nc.vector.tensor_tensor(s1[:, t, :], d[t][c][:].indirect(entries(l3, lo, hi)), y1[t][:, lo:hi], ADD)
-                    nc.vector.tensor_tensor(s2[:, t, :], d[t][c][:].indirect(entries(l4, lo, hi)), y2[t][:, lo:hi], ADD)
-                if t > 0:
-                    u = t - 1
-                    nc.vector.tensor_tensor(big[:, u, :], s1[:, u, :], s2[:, u, :], MAX)
-                    nc.scalar.activation(zb[:, :, u], big[:, u, :], COPY, scale=gain[:, u : u + 1])
-            quantise(zq, zs, zb, lo, hi)
-            for t in range(PACK):
-                for a, b in pieces(lo, hi):
-                    product(h_banks[t], w3d, ws23d, 4, t, zq, zs, a, b)
-                nc.scalar.copy(h[t][:, lo:hi], h_banks[t][:, lo:hi])
+
+        def scale_z(t, lo, hi, big):
+            for part, (a, b) in enumerate(PARTS):
+                if lo <= a and b <= hi:
+                    nc.scalar.activation(zb[part][:, :, t], big[:, a - lo : b - lo], COPY, scale=gain[:, t : t + 1])
+
+        def fetch(window, lst, name):
+            dst = sb.tile([P, S], F32, name=name)
+            nc.vector.tensor_copy(dst[:], window[:].indirect(lst[:]))
+            return dst
+
+        def fetch_with(window, lst, lo, hi, other, op, name):
+            dst = sb.tile([P, hi - lo], F32, name=name)
+            nc.vector.tensor_tensor(dst[:], window[:].indirect(entries(lst, lo, hi)), other, op)
+            return dst
+
+        def add_excess(base, diff, dst, name):
+            excess = sb.tile([P, S], F32, name=name)
+            nc.scalar.activation(excess[:], diff[:], RELU)
+            nc.gpsimd.tensor_tensor(dst, base, excess[:], ADD)
+
+        y1 = [fetch(y[t][0], l1, "y1_%d" % t) for t in range(3)]
+        first = [fetch_with(d[t][0], l3, 0, S, y1[t][:], ADD, "first%d" % t) for t in range(2)]
+        rest = [fetch_with(y[t][0], l2, 0, S, first[t][:], SUB, "rest%d" % t) for t in range(2)]
+        for t in range(2):
+            diff = fetch_with(d[t][0], l4, 0, S, rest[t][:], ADD, "diff%d" % t)
+            big = sb.tile([P, S], F32, name="big%d" % t)
+            add_excess(first[t][:], diff, big[:], "excess%d" % t)
+            scale_z(t, 0, S, big)
+        y2 = {2: fetch(y[2][0], l2, "rest0")}
+        y1.append(fetch(y[3][0], l1, "rest1"))
+        y2[3] = fetch(y[3][0], l2, "d1_%d" % (2 * S))
+
+        def finish_z(t, lo, hi, s1, s2):
+            big = sb.tile([P, hi - lo], F32, name="big%d_%d" % (t, lo))
+            nc.vector.tensor_tensor(big[:], s1[:], s2[:], MAX)
+            scale_z(t, lo, hi, big)
+
+        pending = None
+        for lo, hi in PARTS:
+            for t in (2, 3):
+                window = d[t][-1 if lo else 0]
+                s1 = fetch_with(window, l3, lo, hi, y1[t][:, lo:hi], ADD, "big%d" % (t - 2))
+                if pending:
+                    finish_z(*pending)
+                s2 = fetch_with(window, l4, lo, hi, y2[t][:, lo:hi], ADD, "first%d" % (t - 2))
+                pending = (t, lo, hi, s1, s2)
+        finish_z(*pending)
+        lead = H_ORDER[0]
+        quantise(zq, zs, zb[0], 0, CUT)
+        for a, b in pieces(0, CUT):
+            product(h_banks[lead], w3d, ws3d, 0, lead, zq, zs, a, b)
+        nc.scalar.copy(h[lead][:, 0:CUT], h_banks[lead][:, 0:CUT])
+        quantise(zq, zs, zb[1], CUT, S)
+        last_bank = ps.tile([P, S], F32, name="d_bank0")
+        product(last_bank, w3d, ws3d, 0, lead, zq, zs, CUT, S)
+        nc.vector.tensor_copy(h[lead][:, CUT:S], last_bank[:, CUT:S])
+        for u in H_ORDER[1:]:
+            product(h_banks[u], w3d, ws3d, 0, u, zq, zs, 0, S)
+            nc.scalar.copy(h[u][:, 0:S], h_banks[u][:])
 
         st = [sb.tile([P, S], F32, name="st%d" % t) for t in range(PACK)]
-        h5 = [sb.tile([P, S], F32, name="h5_%d" % t) for t in range(PACK)]
-        for t in range(PACK + 1):
-            if t < PACK:
-                nc.vector.tensor_copy(h5[t][:], h[t][:].indirect(l5[:]))
-            if t > 0:
-                nc.vector.tensor_tensor(st[t - 1][:], h5[t - 1][:], h[t - 1][:, 0:S], MAX)
+        h5 = {}
+        for t in H_ORDER:
+            h5[t] = fetch(h[t], l5, "h5_%d" % t)
+            if t >= 2:
+                diff = sb.tile([P, S], F32, name="h_diff%d" % t)
+                nc.gpsimd.tensor_tensor(diff[:], h5[t][:], h[t][:, 0:S], SUB)
+                add_excess(h[t][:, 0:S], diff, st[t][:], "h_excess%d" % t)
+        for t in range(2):
+            nc.vector.tensor_tensor(st[t][:], h_banks[t][:], h5[t][:], MAX)
 
         oq = sb.tile([P, S], U32, name="oq", align_bytes=64)
         osc = sb.tile([P, S], U8, name="osc", align_bytes=64)
+        ob = [sb.tile([P, hi - lo, PACK], BF16, name="ob%d" % lo, align_bytes=64) for lo, hi in PARTS]
         out_rows = out_0.rearrange("(p t) j -> p t j", t=PACK)
         out_words = out_1[0].rearrange("p n t -> p (n t)").bitcast(I32)
-        for c, (lo, hi) in enumerate(OUT_CHUNKS):
-            width = hi - lo
-            st6 = sb.tile([P, PACK, width], F32, name="st6_%d" % c)
-            res = sb.tile([P, PACK, width], F32, name="res%d" % c)
-            ob = sb.tile([P, width, PACK], BF16, name="ob%d" % c, align_bytes=64)
-            for t in range(PACK + 1):
-                if t < PACK:
-                    nc.vector.tensor_copy(st6[:, t, :], st[t][:].indirect(entries(l6, lo, hi)))
-                if t > 0:
-                    nc.vector.tensor_tensor(res[:, t - 1, :], st6[:, t - 1, :], st[t - 1][:, lo:hi], MIN)
-                if t > 0 and t % 2 == 0:
-                    nc.scalar.copy(ob[:, :, t - 2 : t], res[:, t - 2 : t, :].rearrange("p t c -> p c t"))
-            nc.sync.dma_start(out_rows[:, :, lo:hi], res[:])
-            quantise(oq, osc, ob, lo, hi)
-            nc.sync.dma_start(out_words[:, lo:hi], oq[:, lo:hi].bitcast(I32))
+        res = {}
+
+        def finish_out(t, lo, hi, st6):
+            first = t - t % 2
+            if t == first:
+                res[first, lo] = sb.tile([P, 2, hi - lo], F32, name="res%d_%d" % (first, lo))
+            pair = res[first, lo]
+            nc.vector.tensor_tensor(pair[:, t - first, :], st6[:], st[t][:, lo:hi], MIN)
+            if t == first:
+                return
+            nc.sync.dma_start(out_rows[:, first : first + 2, lo:hi], pair[:])
+            for part, (a, b) in enumerate(PARTS):
+                if lo <= a and b <= hi:
+                    nc.scalar.copy(ob[part][:, :, first : first + 2], pair[:, :, a - lo : b - lo].rearrange("p t c -> p c t"))
+                    if t == PACK - 1:
+                        quantise(oq, osc, ob[part], a, b)
+                        nc.sync.dma_start(out_words[:, a:b], oq[:, a:b].bitcast(I32))
+
+        pending = None
+        for t, lo, hi in OUT_STEPS:
+            st6 = sb.tile([P, hi - lo], F32, name="st6_%d_%d" % (t, lo))
+            nc.vector.tensor_copy(st6[:], st[t][:].indirect(entries(l6, lo, hi)))
+            if pending:
+                finish_out(*pending)
+            pending = (t, lo, hi, st6)
+        finish_out(*pending)
         for q in range(4):
             queue = nc.scalar if q % 2 == 0 else nc.sync
             queue.dma_start(out_2[0, 4 * q : 4 * q + 4, :].bitcast(I32), osc[32 * q : 32 * q + 4, :].bitcast(I32))

from contextlib import ExitStack

import concourse.mybir as mybir

K, T, S, N, H = 512, 2048, 512, 512, 512
FLOPS = 2 * K * H * S * 2 + 2 * H * N * S

F32 = mybir.dt.float32
BF16 = mybir.dt.bfloat16
I32 = mybir.dt.int32
U32 = mybir.dt.uint32
U16 = mybir.dt.uint16
U8 = mybir.dt.uint8
FP8X4 = mybir.dt.float8_e4m3fn_x4
ADD = mybir.AluOpType.add
SUB = mybir.AluOpType.subtract
RELU = mybir.ActivationFunctionType.Relu
MAX = mybir.AluOpType.max
MIN = mybir.AluOpType.min
COPY = mybir.ActivationFunctionType.Copy

P = 128
PACK = 4
PER_COL = 16
CUT = 384
PARTS = ((0, CUT), (CUT, S))
OUT_STEPS = tuple((t, lo, hi) for lo, hi in PARTS for t in range(PACK))
H_ORDER = (2, 3, 0, 1)


def entries(lst, lo, hi):
    return lst[:, lo // PER_COL : hi // PER_COL]


def pieces(lo, hi):
    return [(a, min(a + 256, hi)) for a in range(lo, hi, 256)]


def tile_picked_twlpathbhopmn_none_po_kernel(
    tc, x_words, x_scales, w1_words, w1_scales, w2_words, w2_scales, gn, w3_words, w3_scales,
    offs, two, n1, n2, n3, n4, n5, n6, out_0, out_1, out_2,
):
    nc = tc.nc
    with ExitStack() as ctx:
        sb = ctx.enter_context(tc.tile_pool(name="sb", bufs=1))
        ps = ctx.enter_context(tc.psum_pool(name="ps", bufs=1))

        def load_words(src, width, name):
            dst = sb.tile([P, width], U32, name=name, align_bytes=64)
            nc.sync.dma_start(dst[:].bitcast(I32), src[0].rearrange("p n t -> p (n t)").bitcast(I32))
            return dst

        def load_scale_rows(queue, dst, src, first):
            for q in range(4):
                queue.dma_start(dst[32 * q + first : 32 * q + first + 4, :].bitcast(I32), src[0, 4 * q : 4 * q + 4, :].bitcast(I32))

        def load_list(src, name):
            dst = sb.tile([P, S // PER_COL], U16, name=name)
            nc.sync.dma_start(dst[:], src)
            return dst

        def deal_aside(src, dtype, name):
            dst = sb.tile([P, H], dtype, name=name, align_bytes=64)
            nc.gpsimd.tensor_copy(dst[:].rearrange("p (t m) -> p t m", t=PACK), src[:].rearrange("p (m t) -> p t m", t=PACK))
            return dst

        def deal(src, dtype, name):
            dst = sb.tile([P, H], dtype, name=name, align_bytes=64)
            nc.vector.tensor_copy(dst[:].rearrange("p (t m) -> p m t", t=PACK), src[:].rearrange("p (m t) -> p m t", t=PACK))
            return dst

        xs = sb.tile([P, T], U8, name="xs", align_bytes=64)
        ws1 = sb.tile([P, H], U8, name="ws1", align_bytes=64)
        ws2 = sb.tile([P, H], U8, name="ws2", align_bytes=64)
        ws3 = sb.tile([P, N], U8, name="ws3", align_bytes=64)
        nc.vector.memset(xs[:].bitcast(I32), 0)
        nc.gpsimd.memset(ws1[:].bitcast(I32), 0)
        nc.gpsimd.memset(ws2[:].bitcast(I32), 0)
        nc.gpsimd.memset(ws3[:].bitcast(I32), 0)

        l_offs = load_list(offs, "l_offs")
        w1 = load_words(w1_words, H, "w1")
        l_two = load_list(two, "l_two")
        load_scale_rows(nc.sync, xs, x_scales, 0)
        xw = load_words(x_words, T, "xw")
        load_scale_rows(nc.sync, ws1, w1_scales, 0)
        l1 = load_list(n1, "l1")
        w2 = load_words(w2_words, H, "w2")
        load_scale_rows(nc.sync, ws2, w2_scales, 0)
        l3 = load_list(n3, "l3")
        l2 = load_list(n2, "l2")
        l4 = load_list(n4, "l4")
        gain = sb.tile([P, PACK], F32, name="gain")
        nc.sync.dma_start(gain[:], gn.rearrange("(p t) o -> p (t o)", t=PACK))
        w3 = load_words(w3_words, N, "w3")
        load_scale_rows(nc.sync, ws3, w3_scales, 0)
        l5 = load_list(n5, "l5")
        l6 = load_list(n6, "l6")

        def pick(window, lst, dtype, name):
            dst = sb.tile([P, S], dtype, name=name, align_bytes=64)
            nc.vector.tensor_copy(dst[:], window[:].indirect(lst[:]))
            return dst

        def product(bank, w_codes, w_plane, first, t, codes, plane, lo, hi):
            cols = slice(P * t, P * (t + 1))
            nc.tensor.matmul_mx(
                out=bank[:, lo:hi], lhsT=w_codes[:, cols].bitcast(FP8X4), lhsT_scale=w_plane[first:P, cols],
                rhs=codes[:, lo:hi].bitcast(FP8X4), rhs_scale=plane[:, lo:hi], start=True, stop=True,
            )

        def quantise(codes, plane, woven, lo, hi):
            for a, b in pieces(lo, hi):
                nc.vector.quantize_mx(
                    out=codes[:, a:b].bitcast(FP8X4), scales=plane[:, a:b],
                    in_=woven[:, a - lo : b - lo, :].rearrange("p c t -> p (c t)"),
                )

        def layer(w_codes, w_plane, codes, plane, name, windows):
            rows = []
            for t in range(PACK):
                bank = ps.tile([P, S], F32, name=name + "_bank%d" % t)
                product(bank, w_codes, w_plane, 0, t, codes, plane, 0, S)
                copies = [sb.tile([P, w], F32, name=name + "%d_%d" % (t, w)) for w in windows[t]]
                for row in copies:
                    nc.scalar.copy(row[:, 0:S], bank[:])
                rows.append(copies)
            return rows

        w1d = deal(w1, U32, "w1d")
        xs_a = pick(xs, l_offs, U8, "xs_a")
        xs_b = pick(xs, l_two, U8, "xs_b")
        xw_a = pick(xw, l_offs, U32, "xw_a")
        ws1d = deal_aside(ws1, U8, "ws1d")
        y = layer(w1d, ws1d, xw_a, xs_a, "y", [(2 * S,)] * PACK)
        xw_b = pick(xw, l_two, U32, "xw_b")
        w2d = deal_aside(w2, U32, "w2d")
        ws2d = deal_aside(ws2, U8, "ws2d")
        d = layer(w2d, ws2d, xw_b, xs_b, "d", [(2 * S,), (2 * S,), (2 * S, S), (2 * S, S)])

        w3d = deal_aside(w3, U32, "w3d")
        ws3d = deal_aside(ws3, U8, "ws3d")
        zq = sb.tile([P, S], U32, name="zq", align_bytes=64)
        zs = sb.tile([P, S], U8, name="zs", align_bytes=64)
        zb = [sb.tile([P, hi - lo, PACK], BF16, name="zb%d" % lo, align_bytes=64) for lo, hi in PARTS]
        h_banks = [ps.tile([P, S], F32, name="y_bank%d" % t) for t in range(PACK)]
        h = [sb.tile([P, 2 * S], F32, name="h%d" % t) for t in range(PACK)]

        def scale_z(t, lo, hi, big):
            for part, (a, b) in enumerate(PARTS):
                if lo <= a and b <= hi:
                    nc.scalar.activation(zb[part][:, :, t], big[:, a - lo : b - lo], COPY, scale=gain[:, t : t + 1])

        def fetch(window, lst, name):
            dst = sb.tile([P, S], F32, name=name)
            nc.vector.tensor_copy(dst[:], window[:].indirect(lst[:]))
            return dst

        def fetch_with(window, lst, lo, hi, other, op, name):
            dst = sb.tile([P, hi - lo], F32, name=name)
            nc.vector.tensor_tensor(dst[:], window[:].indirect(entries(lst, lo, hi)), other, op)
            return dst

        def add_excess(base, diff, dst, name):
            excess = sb.tile([P, S], F32, name=name)
            nc.scalar.activation(excess[:], diff[:], RELU)
            nc.gpsimd.tensor_tensor(dst, base, excess[:], ADD)

        y1 = [fetch(y[t][0], l1, "y1_%d" % t) for t in range(3)]
        first = [fetch_with(d[t][0], l3, 0, S, y1[t][:], ADD, "first%d" % t) for t in range(2)]
        rest = [fetch_with(y[t][0], l2, 0, S, first[t][:], SUB, "rest%d" % t) for t in range(2)]
        for t in range(2):
            diff = fetch_with(d[t][0], l4, 0, S, rest[t][:], ADD, "diff%d" % t)
            big = sb.tile([P, S], F32, name="big%d" % t)
            add_excess(first[t][:], diff, big[:], "excess%d" % t)
            scale_z(t, 0, S, big)
        y2 = {2: fetch(y[2][0], l2, "rest0")}
        y1.append(fetch(y[3][0], l1, "rest1"))
        y2[3] = fetch(y[3][0], l2, "d1_%d" % (2 * S))

        def finish_z(t, lo, hi, s1, s2):
            big = sb.tile([P, hi - lo], F32, name="big%d_%d" % (t, lo))
            nc.vector.tensor_tensor(big[:], s1[:], s2[:], MAX)
            scale_z(t, lo, hi, big)

        pending = None
        for lo, hi in PARTS:
            for t in (2, 3):
                window = d[t][-1 if lo else 0]
                s1 = fetch_with(window, l3, lo, hi, y1[t][:, lo:hi], ADD, "big%d" % (t - 2))
                if pending:
                    finish_z(*pending)
                s2 = fetch_with(window, l4, lo, hi, y2[t][:, lo:hi], ADD, "first%d" % (t - 2))
                pending = (t, lo, hi, s1, s2)
        finish_z(*pending)
        lead = H_ORDER[0]
        quantise(zq, zs, zb[0], 0, CUT)
        for a, b in pieces(0, CUT):
            product(h_banks[lead], w3d, ws3d, 0, lead, zq, zs, a, b)
        nc.scalar.copy(h[lead][:, 0:CUT], h_banks[lead][:, 0:CUT])
        quantise(zq, zs, zb[1], CUT, S)
        last_bank = ps.tile([P, S], F32, name="d_bank0")
        product(last_bank, w3d, ws3d, 0, lead, zq, zs, CUT, S)
        nc.vector.tensor_copy(h[lead][:, CUT:S], last_bank[:, CUT:S])
        for u in H_ORDER[1:]:
            product(h_banks[u], w3d, ws3d, 0, u, zq, zs, 0, S)
            nc.scalar.copy(h[u][:, 0:S], h_banks[u][:])

        st = [sb.tile([P, S], F32, name="st%d" % t) for t in range(PACK)]
        h5 = {}
        for t in H_ORDER:
            h5[t] = fetch(h[t], l5, "h5_%d" % t)
            if t >= 2:
                diff = sb.tile([P, S], F32, name="h_diff%d" % t)
                nc.gpsimd.tensor_tensor(diff[:], h5[t][:], h[t][:, 0:S], SUB)
                add_excess(h[t][:, 0:S], diff, st[t][:], "h_excess%d" % t)
        for t in range(2):
            nc.vector.tensor_tensor(st[t][:], h_banks[t][:], h5[t][:], MAX)

        oq = sb.tile([P, S], U32, name="oq", align_bytes=64)
        osc = sb.tile([P, S], U8, name="osc", align_bytes=64)
        ob = [sb.tile([P, hi - lo, PACK], BF16, name="ob%d" % lo, align_bytes=64) for lo, hi in PARTS]
        out_rows = out_0.rearrange("(p t) j -> p t j", t=PACK)
        out_words = out_1[0].rearrange("p n t -> p (n t)").bitcast(I32)
        res = {}

        def finish_out(t, lo, hi, st6):
            first = t - t % 2
            if t == first:
                res[first, lo] = sb.tile([P, 2, hi - lo], F32, name="res%d_%d" % (first, lo))
            pair = res[first, lo]
            nc.vector.tensor_tensor(pair[:, t - first, :], st6[:], st[t][:, lo:hi], MIN)
            if t == first:
                return
            nc.sync.dma_start(out_rows[:, first : first + 2, lo:hi], pair[:])
            for part, (a, b) in enumerate(PARTS):
                if lo <= a and b <= hi:
                    nc.scalar.copy(ob[part][:, :, first : first + 2], pair[:, :, a - lo : b - lo].rearrange("p t c -> p c t"))
                    if t == PACK - 1:
                        quantise(oq, osc, ob[part], a, b)
                        nc.sync.dma_start(out_words[:, a:b], oq[:, a:b].bitcast(I32))

        pending = None
        for t, lo, hi in OUT_STEPS:
            st6 = sb.tile([P, hi - lo], F32, name="st6_%d_%d" % (t, lo))
            nc.vector.tensor_copy(st6[:], st[t][:].indirect(entries(l6, lo, hi)))
            if pending:
                finish_out(*pending)
            pending = (t, lo, hi, st6)
        finish_out(*pending)
        for q in range(4):
            queue = nc.scalar if q % 2 == 0 else nc.sync
            queue.dma_start(out_2[0, 4 * q : 4 * q + 4, :].bitcast(I32), osc[32 * q : 32 * q + 4, :].bitcast(I32))
